import numpy as np, ml_dtypes
CORES = [8,80,112,136,208,240,264,336,368,392,464,496]
N = 12
import mx_ref
NC = 128
CNT = [[0,0,16,0,24,4,18,0,32,0,12,22],[12,0,14,0,14,42,0,6,0,16,2,22],[10,14,0,26,36,0,30,0,2,0,10,0],[0,42,14,0,6,2,4,26,28,6,0,0],[0,4,2,10,0,38,12,0,6,18,38,0],[54,0,0,0,6,0,16,0,22,14,16,0],[6,34,0,36,22,0,0,10,16,4,0,0],[0,2,30,6,0,14,0,0,14,38,20,4],[16,8,4,14,0,12,2,0,0,30,0,42],[14,6,30,6,16,0,0,6,8,0,18,24],[10,6,18,30,4,0,24,22,0,0,0,14],[6,12,0,0,0,16,22,58,0,2,12,0]]
OFF = [[sum(c[:e]) for e in range(N + 1)] for c in CNT]
BF = ml_dtypes.bfloat16
def setup_inputs(rng):
    def f(*shape):
        return mx_ref.flush((rng.standard_normal(shape, dtype=np.float32) * np.exp2(rng.integers(-2, 3, shape[:-1] + (1,)))).astype(BF))
    return {"w": f(N, 128, 512), "x": f(N, 128, 4 * NC)}
def setup_inputs_blocks(rng):
    d = setup_inputs(rng)
    for k in ("w", "x"): d[k] = mx_ref.spread(d[k], rng, 4)
    return d
def setup_inputs_wide(rng):
    d = setup_inputs(rng)
    for k in ("w", "x"): d[k] = mx_ref.flush((d[k].astype(np.float32) * np.exp2(rng.integers(-8, 9, (N, 1, 1))).astype(np.float32)).astype(BF))
    return d
def setup_inputs_zeros(rng):
    d = setup_inputs(rng); v = d["x"].reshape(N, 128, -1, 4).copy()
    v[np.broadcast_to((rng.random((N, 1, v.shape[2], 1)) < 0.33), v.shape)] = 0
    d["x"] = v.reshape(d["x"].shape)
    return d
def reference(w, x):
    y = np.zeros((N, 128, NC), np.float32)
    for e in range(N):
        t = np.concatenate([x[j][:, 4 * OFF[j][e]:4 * OFF[j][e + 1]] for j in range(N)], axis=1)
        y[e] = mx_ref.matmul(mx_ref.quantize(w[e]), mx_ref.quantize(t))
    return {"y": y}

@@ -1,0 +1,202 @@
+from concourse.bass import DstId, RemoteDMATransfer
+from concourse.mybir import dt
+
+NC = 128
+LAND = 256
+HOSTS = 4
+
+EF_ON, EF_OFF, ES = 8, 8, 8
+RELAY_LAG = 64
+
+SCRATCH = {
+    "xb": ("sbuf", [128, 4 * NC], "bfloat16"),
+    "wb": ("sbuf", [128, 4 * NC], "bfloat16"),
+    "q": ("sbuf", [128, NC], "float8_e4m3fn_x4"),
+    "s": ("sbuf", [128, NC], "uint8"),
+    "wq": ("sbuf", [128, NC], "float8_e4m3fn_x4"),
+    "ws": ("sbuf", [128, NC], "uint8"),
+    "lq": ("sbuf", [128, LAND], "float8_e4m3fn_x4"),
+    "ls": ("sbuf", [128, LAND], "uint8"),
+    "yb": ("sbuf", [128, NC], "float32"),
+    "ps": ("psum", [128, 512], "float32"),
+}
+SEMAPHORES = ["ldx", "ldw", "qx", "qw", "fed", "sent", "arr", "mm", "cp", "st"]
+
+_CACHE = {}
+
+
+def _p2(d):
+    p = 1
+    while p < d:
+        p *= 2
+    return p
+
+
+def _product(opts):
+    out = [[]]
+    for o in opts:
+        out = [p + [k] for p in out for k in o]
+    return out
+
+
+def _bits(mask):
+    return [i for i in range(16) if (mask >> i) & 1]
+
+
+def _plan(T, topo):
+    if "p" in _CACHE:
+        return _CACHE["p"]
+    cores = list(T.cores)
+    cnt = T.tables["CNT"]
+    n = len(cores)
+    world = range(HOSTS * topo.CORES_PER_HOST)
+    off = [[sum(r[:e]) for e in range(n + 1)] for r in cnt]
+
+    def reach(c):
+        return sum(1 for d in cores if d != c and topo.may_write(c, d))
+
+    relay = {}
+    groups = {}
+    for j in range(n):
+        c0 = cores[j]
+        h = topo.host(c0)
+        same = [c for c in world if c != c0 and topo.host(c) == h and topo.chip(c) == topo.chip(c0)]
+        a = sorted(same, key=lambda c: (-reach(c), topo.die(c) != topo.die(c0), c))[:2]
+        hb = [x for x in range(HOSTS) if x != h and topo.rack(x) == topo.rack(h)][0]
+        far = [c for c in world if topo.host(c) == hb and topo.chip(c) == topo.chip(c0) and c not in cores
+               and topo.may_write(c0, c)]
+        b = sorted(far, key=lambda c: (-reach(c), topo.die(c) == topo.die(c0), c))[:2]
+        relay[(j, "A")], relay[(j, "B")] = a, b
+        dests = [e for e in range(n) if e != j and cnt[j][e] > 0]
+        opts = []
+        for e in dests:
+            d = cores[e]
+            opts.append([k for k, cs in (("Z", [c0]), ("A", a), ("B", b)) if all(topo.may_write(c, d) for c in cs)])
+        best = None
+        for ch in _product(opts):
+            g = {k: [e for e, c in zip(dests, ch) if c == k] for k in "ZAB"}
+            t = [32 + 32 * _p2(len(g["Z"])) if g["Z"] else 0,
+                 32 + RELAY_LAG + 16 * _p2(len(g["A"])) if g["A"] else 0,
+                 40 + RELAY_LAG + 16 * _p2(len(g["B"])) if g["B"] else 0]
+            pad = sum(max(cnt[j][e] for e in v) * len(v) for v in g.values() if v)
+            key = (max(t), sum(t), pad)
+            if best is None or key < best[0]:
+                best = (key, g)
+        for k, v in best[1].items():
+            groups[(j, k)] = v
+
+    width = {}
+    for (j, k), v in groups.items():
+        for e in v:
+            width[(j, e)] = max(cnt[j][x] for x in v)
+    win = {}
+    ranks = []
+    for e in range(n):
+        srcs = [j for j in range(n) if (j, e) in width]
+        best = None
+        for ends in _product([[0, 1]] * len(srcs)):
+            pos, wins, merged = 0, [], []
+            for j, right in zip(srcs, ends):
+                w, c, o = width[(j, e)], cnt[j][e], off[j][e]
+                a0 = min(max(o + c - w if right else o, 0), NC - w)
+                wins.append((j, a0, pos, w))
+                p = [pos + o - a0, sum(cnt[x][e] for x in range(j)), c]
+                if merged and merged[-1][0] + merged[-1][2] == p[0] and merged[-1][1] + merged[-1][2] == p[1]:
+                    merged[-1][2] += c
+                else:
+                    merged.append(p)
+                pos += w
+            if best is None or len(merged) < len(best[1]):
+                best = (wins, merged, pos)
+        for j, a0, pos, w in best[0]:
+            win[(j, e)] = (a0, pos, w)
+        assert NC <= best[2] <= LAND and best[2] % 2 == 0
+        ranks.append({"cols": best[2], "copies": best[1], "arrive": 0})
+
+    calls = {}
+    waits = {}
+    for j in range(n):
+        c0 = cores[j]
+        mine = calls.setdefault(c0, [])
+        for kind in (0, 1):
+            feed = []
+            for k, ne in (("A", EF_ON), ("B", EF_OFF)):
+                if not groups[(j, k)]:
+                    continue
+                r = relay[(j, k)][kind]
+                eng = _bits(topo.mask(c0, r))
+                if k == "A":
+                    away = _bits(topo.mask(c0, relay[(j, "B")][kind]))
+                    eng = [x for x in eng if x not in away] + [x for x in eng if x in away]
+                eng = eng[:ne]
+                feed.append((r, 0, 0, NC, eng, True))
+                assert r not in waits and r not in cores
+                waits[r] = len(eng)
+            if feed:
+                mine.append((kind, feed))
+        for k in "ZAB":
+            v = groups[(j, k)]
+            if not v:
+                continue
+            for kind in (0, 1):
+                src = c0 if k == "Z" else relay[(j, k)][kind]
+                each = ES // _p2(len(v))
+                items = []
+                for i, e in enumerate(v):
+                    eng = _bits(topo.mask(src, cores[e]))[i * each:(i + 1) * each]
+                    assert len(eng) == each
+                    a0, pos, w = win[(j, e)]
+                    items.append((cores[e], a0, pos, w, eng, False))
+                    ranks[e]["arrive"] += each
+                calls.setdefault(src, []).append((kind, items))
+    _CACHE["p"] = (ranks, calls, waits)
+    return _CACHE["p"]
+
+
+def _issue(g, T, topo, core, calls):
+    left = 0
+    for kind, items in calls:
+        ts = []
+        for d, a0, pos, w, eng, feed in items:
+            rid, pid = topo.addr(d, core)
+            if kind == 0:
+                src = T.q[:, a0:a0 + w].bitcast(dt.uint8)
+                dst = (T.q if feed else T.lq)[:, pos:pos + w].bitcast(dt.uint8)
+            else:
+                src = T.s[:, a0:a0 + w]
+                dst = (T.s if feed else T.ls)[:, pos:pos + w]
+            ts.append(RemoteDMATransfer(dst_ids=[DstId(rid=rid, pnc=pid)], dma_engine_mask=sum(1 << x for x in eng),
+                                        remote_sem=T.sem.fed if feed else T.sem.arr, src=src, dst=dst))
+            left += len(eng)
+        g.remote_dma_fused(ts, local_sem=T.sem.sent)
+    return left
+
+
+def rank_program(g, core, T, topo):
+    ranks, calls, waits = _plan(T, topo)
+    rank = T.rank_of(core)
+    if rank is None:
+        if core in waits:
+            g.wait_ge(T.sem.fed, waits[core])
+            g.wait_ge(T.sem.sent, _issue(g, T, topo, core, calls[core]))
+        return
+    me = ranks[rank]
+    g.sync.dma_start(T.xb[:, :], T.x[:, :]).then_inc(T.sem.ldx, 16)
+    g.sync.dma_start(T.wb[:, :], T.w[:, :]).then_inc(T.sem.ldw, 16)
+    g.vector.wait_ge(T.sem.ldx, 16)
+    g.vector.quantize_mx(T.q[:, :], T.s[:, :], T.xb[:, :]).then_inc(T.sem.qx, 1)
+    g.vector.wait_ge(T.sem.ldw, 16)
+    g.vector.quantize_mx(T.wq[:, :], T.ws[:, :], T.wb[:, :]).then_inc(T.sem.qw, 1)
+    g.wait_ge(T.sem.qx, 1)
+    left = _issue(g, T, topo, core, calls[core])
+    n = me["cols"]
+    g.tensor.wait_ge(T.sem.qw, 1)
+    g.tensor.wait_ge(T.sem.arr, me["arrive"])
+    g.tensor.matmul_mx(T.ps[:, 0:n], T.wq[:, :], T.ws[:, :], T.lq[:, 0:n], T.ls[:, 0:n], True, True).then_inc(T.sem.mm, 1)
+    g.vector.wait_ge(T.sem.mm, 1)
+    for p, yo, c in me["copies"]:
+        g.vector.tensor_copy(T.yb[:, yo:yo + c], T.ps[:, p:p + c]).then_inc(T.sem.cp, 1)
+    g.sync.wait_ge(T.sem.cp, len(me["copies"]))
+    g.sync.dma_start(T.y[:, :], T.yb[:, :]).then_inc(T.sem.st, 16)
+    g.sync.wait_ge(T.sem.st, 16)
+    g.wait_ge(T.sem.sent, left)

@@ -3,10 +3,14 @@ from concourse.mybir import dt
 
 NC = 128
 LAND = 256
+BANK = 512
 HOSTS = 4
 
-EF_ON, EF_OFF, ES = 8, 8, 8
+EF = 4
+ES = 8
+EC = 4
 RELAY_LAG = 64
+SHORT = 64
 
 SCRATCH = {
     "xb": ("sbuf", [128, 4 * NC], "bfloat16"),
@@ -18,7 +22,7 @@ SCRATCH = {
     "lq": ("sbuf", [128, LAND], "float8_e4m3fn_x4"),
     "ls": ("sbuf", [128, LAND], "uint8"),
     "yb": ("sbuf", [128, NC], "float32"),
-    "ps": ("psum", [128, 512], "float32"),
+    "ps": ("psum", [128, BANK], "float32"),
 }
 SEMAPHORES = ["ldx", "ldw", "qx", "qw", "fed", "sent", "arr", "mm", "cp", "st"]
 
@@ -43,6 +47,22 @@ def _bits(mask):
     return [i for i in range(16) if (mask >> i) & 1]
 
 
+def _splits(k, v, row):
+    per = max(1, EC * _p2(len(v)) // ES)
+    if k == "Z" or per == 1:
+        return [[[e] for e in v]]
+    if per == 2:
+        out = []
+        for x in v[1:]:
+            rest = [e for e in v[1:] if e != x]
+            out.append([[v[0], x], rest])
+        if len(v) == 3:
+            out.append([[v[1], v[2]], [v[0]]])
+        return out
+    w = sorted(v, key=lambda e: -row[e])
+    return [[w[i:i + per] for i in range(0, len(w), per)]]
+
+
 def _plan(T, topo):
     if "p" in _CACHE:
         return _CACHE["p"]
@@ -55,6 +75,9 @@ def _plan(T, topo):
     def reach(c):
         return sum(1 for d in cores if d != c and topo.may_write(c, d))
 
+    def far(c, d):
+        return topo.rack(topo.host(c)) != topo.rack(topo.host(d))
+
     relay = {}
     groups = {}
     for j in range(n):
@@ -63,9 +86,9 @@ def _plan(T, topo):
         same = [c for c in world if c != c0 and topo.host(c) == h and topo.chip(c) == topo.chip(c0)]
         a = sorted(same, key=lambda c: (-reach(c), topo.die(c) != topo.die(c0), c))[:2]
         hb = [x for x in range(HOSTS) if x != h and topo.rack(x) == topo.rack(h)][0]
-        far = [c for c in world if topo.host(c) == hb and topo.chip(c) == topo.chip(c0) and c not in cores
-               and topo.may_write(c0, c)]
-        b = sorted(far, key=lambda c: (-reach(c), topo.die(c) == topo.die(c0), c))[:2]
+        away = [c for c in world if topo.host(c) == hb and topo.chip(c) == topo.chip(c0) and c not in cores
+                and topo.may_write(c0, c)]
+        b = sorted(away, key=lambda c: (-reach(c), topo.die(c) == topo.die(c0), c))[:2]
         relay[(j, "A")], relay[(j, "B")] = a, b
         dests = [e for e in range(n) if e != j and cnt[j][e] > 0]
         opts = []
@@ -78,27 +101,31 @@ def _plan(T, topo):
             t = [32 + 32 * _p2(len(g["Z"])) if g["Z"] else 0,
                  32 + RELAY_LAG + 16 * _p2(len(g["A"])) if g["A"] else 0,
                  40 + RELAY_LAG + 16 * _p2(len(g["B"])) if g["B"] else 0]
-            pad = sum(max(cnt[j][e] for e in v) * len(v) for v in g.values() if v)
-            key = (max(t), sum(t), pad)
+            cols = 0
+            for k, v in g.items():
+                if v and k != "Z":
+                    cols += (2 if k == "B" else 1) * (off[j][max(v) + 1] - off[j][min(v)])
+                    cols += min(sum(max(cnt[j][e] for e in p) * len(p) for p in sp) for sp in _splits(k, v, cnt[j]))
+            key = (max(t), sum(t), cols)
             if best is None or key < best[0]:
                 best = (key, g)
         for k, v in best[1].items():
-            groups[(j, k)] = v
+            if v:
+                groups[(j, k)] = v
+    hull = {(j, k): (0, NC) if k == "Z" else (off[j][min(v)], off[j][max(v) + 1]) for (j, k), v in groups.items()}
 
-    width = {}
-    for (j, k), v in groups.items():
-        for e in v:
-            width[(j, e)] = max(cnt[j][x] for x in v)
-    win = {}
-    ranks = []
-    for e in range(n):
-        srcs = [j for j in range(n) if (j, e) in width]
+    memo = {}
+
+    def strip(e, ws):
+        key = (e, tuple(ws))
+        if key in memo:
+            return memo[key]
         best = None
-        for ends in _product([[0, 1]] * len(srcs)):
+        for ends in _product([[0, 1] if w > cnt[j][e] else [0] for j, w, hl in ws]):
             pos, wins, merged = 0, [], []
-            for j, right in zip(srcs, ends):
-                w, c, o = width[(j, e)], cnt[j][e], off[j][e]
-                a0 = min(max(o + c - w if right else o, 0), NC - w)
+            for (j, w, (lo, hi)), right in zip(ws, ends):
+                c, o = cnt[j][e], off[j][e]
+                a0 = min(max(o + c - w if right else o, lo), hi - w)
                 wins.append((j, a0, pos, w))
                 p = [pos + o - a0, sum(cnt[x][e] for x in range(j)), c]
                 if merged and merged[-1][0] + merged[-1][2] == p[0] and merged[-1][1] + merged[-1][2] == p[1]:
@@ -106,49 +133,84 @@ def _plan(T, topo):
                 else:
                     merged.append(p)
                 pos += w
-            if best is None or len(merged) < len(best[1]):
-                best = (wins, merged, pos)
-        for j, a0, pos, w in best[0]:
+            cost = pos + sum(max(SHORT, m[2]) for m in merged)
+            if best is None or cost < best[0]:
+                best = (cost, wins, merged, pos)
+        memo[key] = best
+        return best
+
+    def strips(parts):
+        width = {}
+        for (j, k), sp in parts.items():
+            for p in sp:
+                for e in p:
+                    width[(j, e)] = (max(cnt[j][x] for x in p), hull[(j, k)])
+        return [strip(e, [(j,) + width[(j, e)] for j in range(n) if (j, e) in width]) for e in range(n)]
+
+    def score(parts):
+        c = sorted((r[0] for r in strips(parts)), reverse=True)
+        return c
+
+    ways = {gk: _splits(gk[1], v, cnt[gk[0]]) for gk, v in groups.items()}
+    parts = {gk: min(w, key=lambda sp: sum(max(cnt[gk[0]][e] for e in p) * len(p) for p in sp)) for gk, w in ways.items()}
+    now = score(parts)
+    for sweep in range(4):
+        moved = False
+        for gk in sorted(ways):
+            for sp in ways[gk]:
+                trial = dict(parts)
+                trial[gk] = sp
+                sc = score(trial)
+                if sc < now:
+                    parts, now, moved = trial, sc, True
+        if not moved:
+            break
+    win = {}
+    ranks = []
+    for e, (cost, wins, merged, cols) in enumerate(strips(parts)):
+        for j, a0, pos, w in wins:
             win[(j, e)] = (a0, pos, w)
-        assert NC <= best[2] <= LAND and best[2] % 2 == 0
-        ranks.append({"cols": best[2], "copies": best[1], "arrive": 0})
+        assert NC <= cols <= LAND and cols % 2 == 0
+        ranks.append({"cols": cols, "copies": merged, "arrive": 0})
 
     calls = {}
     waits = {}
     for j in range(n):
         c0 = cores[j]
         mine = calls.setdefault(c0, [])
+        out = _bits(topo.mask(c0, relay[(j, "B")][0]))
         for kind in (0, 1):
-            feed = []
-            for k, ne in (("A", EF_ON), ("B", EF_OFF)):
-                if not groups[(j, k)]:
+            for k in "BA":
+                if (j, k) not in groups:
                     continue
+                lo, hi = hull[(j, k)]
                 r = relay[(j, k)][kind]
                 eng = _bits(topo.mask(c0, r))
                 if k == "A":
-                    away = _bits(topo.mask(c0, relay[(j, "B")][kind]))
-                    eng = [x for x in eng if x not in away] + [x for x in eng if x in away]
-                eng = eng[:ne]
-                feed.append((r, 0, 0, NC, eng, True))
-                assert r not in waits and r not in cores
+                    eng = [x for x in eng if x not in out] + [x for x in eng if x in out]
+                eng = eng[kind:2 * EF:2]
+                assert len(eng) == EF and r not in waits and r not in cores
+                mine.append((kind, [(r, lo, lo, hi - lo, eng, "fed")]))
                 waits[r] = len(eng)
-            if feed:
-                mine.append((kind, feed))
         for k in "ZAB":
-            v = groups[(j, k)]
-            if not v:
+            if (j, k) not in groups:
                 continue
-            for kind in (0, 1):
-                src = c0 if k == "Z" else relay[(j, k)][kind]
-                each = ES // _p2(len(v))
-                items = []
-                for i, e in enumerate(v):
-                    eng = _bits(topo.mask(src, cores[e]))[i * each:(i + 1) * each]
-                    assert len(eng) == each
-                    a0, pos, w = win[(j, e)]
-                    items.append((cores[e], a0, pos, w, eng, False))
-                    ranks[e]["arrive"] += each
-                calls.setdefault(src, []).append((kind, items))
+            first = c0 if k == "Z" else relay[(j, k)][0]
+            sp = sorted(parts[(j, k)], key=lambda p: (not any(far(first, cores[e]) for e in p), -max(cnt[j][e] for e in p)))
+            room = ES // _p2(len(sp))
+            for i, p in enumerate(sp):
+                each = room // _p2(len(p))
+                for kind in (0, 1):
+                    src = c0 if k == "Z" else relay[(j, k)][kind]
+                    items = []
+                    for m, e in enumerate(p):
+                        lo = i * room + m * each
+                        eng = _bits(topo.mask(src, cores[e]))[lo:lo + each]
+                        assert len(eng) == each
+                        a0, pos, w = win[(j, e)]
+                        items.append((cores[e], a0, pos, w, eng, "arr"))
+                        ranks[e]["arrive"] += each
+                    calls.setdefault(src, []).append((kind, items))
     _CACHE["p"] = (ranks, calls, waits)
     return _CACHE["p"]
 
@@ -157,8 +219,9 @@ def _issue(g, T, topo, core, calls):
     left = 0
     for kind, items in calls:
         ts = []
-        for d, a0, pos, w, eng, feed in items:
+        for d, a0, pos, w, eng, mark in items:
             rid, pid = topo.addr(d, core)
+            feed = mark == "fed"
             if kind == 0:
                 src = T.q[:, a0:a0 + w].bitcast(dt.uint8)
                 dst = (T.q if feed else T.lq)[:, pos:pos + w].bitcast(dt.uint8)
@@ -166,7 +229,7 @@ def _issue(g, T, topo, core, calls):
                 src = T.s[:, a0:a0 + w]
                 dst = (T.s if feed else T.ls)[:, pos:pos + w]
             ts.append(RemoteDMATransfer(dst_ids=[DstId(rid=rid, pnc=pid)], dma_engine_mask=sum(1 << x for x in eng),
-                                        remote_sem=T.sem.fed if feed else T.sem.arr, src=src, dst=dst))
+                                        remote_sem=T.sem[mark], src=src, dst=dst))
             left += len(eng)
         g.remote_dma_fused(ts, local_sem=T.sem.sent)
     return left

from concourse.bass import DstId, RemoteDMATransfer
from concourse.mybir import dt

NC = 128
LAND = 256
BANK = 512
HOSTS = 4

EF = 4
ES = 8
EC = 4
RELAY_LAG = 64
SHORT = 64

SCRATCH = {
    "xb": ("sbuf", [128, 4 * NC], "bfloat16"),
    "wb": ("sbuf", [128, 4 * NC], "bfloat16"),
    "q": ("sbuf", [128, NC], "float8_e4m3fn_x4"),
    "s": ("sbuf", [128, NC], "uint8"),
    "wq": ("sbuf", [128, NC], "float8_e4m3fn_x4"),
    "ws": ("sbuf", [128, NC], "uint8"),
    "lq": ("sbuf", [128, LAND], "float8_e4m3fn_x4"),
    "ls": ("sbuf", [128, LAND], "uint8"),
    "yb": ("sbuf", [128, NC], "float32"),
    "ps": ("psum", [128, BANK], "float32"),
}
SEMAPHORES = ["ldx", "ldw", "qx", "qw", "fed", "sent", "arr", "mm", "cp", "st"]

_CACHE = {}


def _p2(d):
    p = 1
    while p < d:
        p *= 2
    return p


def _product(opts):
    out = [[]]
    for o in opts:
        out = [p + [k] for p in out for k in o]
    return out


def _bits(mask):
    return [i for i in range(16) if (mask >> i) & 1]


def _splits(k, v, row):
    per = max(1, EC * _p2(len(v)) // ES)
    if k == "Z" or per == 1:
        return [[[e] for e in v]]
    if per == 2:
        out = []
        for x in v[1:]:
            rest = [e for e in v[1:] if e != x]
            out.append([[v[0], x], rest])
        if len(v) == 3:
            out.append([[v[1], v[2]], [v[0]]])
        return out
    w = sorted(v, key=lambda e: -row[e])
    return [[w[i:i + per] for i in range(0, len(w), per)]]


def _plan(T, topo):
    if "p" in _CACHE:
        return _CACHE["p"]
    cores = list(T.cores)
    cnt = T.tables["CNT"]
    n = len(cores)
    world = range(HOSTS * topo.CORES_PER_HOST)
    off = [[sum(r[:e]) for e in range(n + 1)] for r in cnt]

    def reach(c):
        return sum(1 for d in cores if d != c and topo.may_write(c, d))

    def far(c, d):
        return topo.rack(topo.host(c)) != topo.rack(topo.host(d))

    relay = {}
    groups = {}
    for j in range(n):
        c0 = cores[j]
        h = topo.host(c0)
        same = [c for c in world if c != c0 and topo.host(c) == h and topo.chip(c) == topo.chip(c0)]
        a = sorted(same, key=lambda c: (-reach(c), topo.die(c) != topo.die(c0), c))[:2]
        hb = [x for x in range(HOSTS) if x != h and topo.rack(x) == topo.rack(h)][0]
        away = [c for c in world if topo.host(c) == hb and topo.chip(c) == topo.chip(c0) and c not in cores
                and topo.may_write(c0, c)]
        b = sorted(away, key=lambda c: (-reach(c), topo.die(c) == topo.die(c0), c))[:2]
        relay[(j, "A")], relay[(j, "B")] = a, b
        dests = [e for e in range(n) if e != j and cnt[j][e] > 0]
        opts = []
        for e in dests:
            d = cores[e]
            opts.append([k for k, cs in (("Z", [c0]), ("A", a), ("B", b)) if all(topo.may_write(c, d) for c in cs)])
        best = None
        for ch in _product(opts):
            g = {k: [e for e, c in zip(dests, ch) if c == k] for k in "ZAB"}
            t = [32 + 32 * _p2(len(g["Z"])) if g["Z"] else 0,
                 32 + RELAY_LAG + 16 * _p2(len(g["A"])) if g["A"] else 0,
                 40 + RELAY_LAG + 16 * _p2(len(g["B"])) if g["B"] else 0]
            cols = 0
            for k, v in g.items():
                if v and k != "Z":
                    cols += (2 if k == "B" else 1) * (off[j][max(v) + 1] - off[j][min(v)])
                    cols += min(sum(max(cnt[j][e] for e in p) * len(p) for p in sp) for sp in _splits(k, v, cnt[j]))
            key = (max(t), sum(t), cols)
            if best is None or key < best[0]:
                best = (key, g)
        for k, v in best[1].items():
            if v:
                groups[(j, k)] = v
    hull = {(j, k): (0, NC) if k == "Z" else (off[j][min(v)], off[j][max(v) + 1]) for (j, k), v in groups.items()}

    memo = {}

    def strip(e, ws):
        key = (e, tuple(ws))
        if key in memo:
            return memo[key]
        best = None
        for ends in _product([[0, 1] if w > cnt[j][e] else [0] for j, w, hl in ws]):
            pos, wins, merged = 0, [], []
            for (j, w, (lo, hi)), right in zip(ws, ends):
                c, o = cnt[j][e], off[j][e]
                a0 = min(max(o + c - w if right else o, lo), hi - w)
                wins.append((j, a0, pos, w))
                p = [pos + o - a0, sum(cnt[x][e] for x in range(j)), c]
                if merged and merged[-1][0] + merged[-1][2] == p[0] and merged[-1][1] + merged[-1][2] == p[1]:
                    merged[-1][2] += c
                else:
                    merged.append(p)
                pos += w
            cost = pos + sum(max(SHORT, m[2]) for m in merged)
            if best is None or cost < best[0]:
                best = (cost, wins, merged, pos)
        memo[key] = best
        return best

    def strips(parts):
        width = {}
        for (j, k), sp in parts.items():
            for p in sp:
                for e in p:
                    width[(j, e)] = (max(cnt[j][x] for x in p), hull[(j, k)])
        return [strip(e, [(j,) + width[(j, e)] for j in range(n) if (j, e) in width]) for e in range(n)]

    def score(parts):
        c = sorted((r[0] for r in strips(parts)), reverse=True)
        return c

    ways = {gk: _splits(gk[1], v, cnt[gk[0]]) for gk, v in groups.items()}
    parts = {gk: min(w, key=lambda sp: sum(max(cnt[gk[0]][e] for e in p) * len(p) for p in sp)) for gk, w in ways.items()}
    now = score(parts)
    for sweep in range(4):
        moved = False
        for gk in sorted(ways):
            for sp in ways[gk]:
                trial = dict(parts)
                trial[gk] = sp
                sc = score(trial)
                if sc < now:
                    parts, now, moved = trial, sc, True
        if not moved:
            break
    win = {}
    ranks = []
    for e, (cost, wins, merged, cols) in enumerate(strips(parts)):
        for j, a0, pos, w in wins:
            win[(j, e)] = (a0, pos, w)
        assert NC <= cols <= LAND and cols % 2 == 0
        ranks.append({"cols": cols, "copies": merged, "arrive": 0})

    calls = {}
    waits = {}
    for j in range(n):
        c0 = cores[j]
        mine = calls.setdefault(c0, [])
        out = _bits(topo.mask(c0, relay[(j, "B")][0]))
        for kind in (0, 1):
            for k in "BA":
                if (j, k) not in groups:
                    continue
                lo, hi = hull[(j, k)]
                r = relay[(j, k)][kind]
                eng = _bits(topo.mask(c0, r))
                if k == "A":
                    eng = [x for x in eng if x not in out] + [x for x in eng if x in out]
                eng = eng[kind:2 * EF:2]
                assert len(eng) == EF and r not in waits and r not in cores
                mine.append((kind, [(r, lo, lo, hi - lo, eng, "fed")]))
                waits[r] = len(eng)
        for k in "ZAB":
            if (j, k) not in groups:
                continue
            first = c0 if k == "Z" else relay[(j, k)][0]
            sp = sorted(parts[(j, k)], key=lambda p: (not any(far(first, cores[e]) for e in p), -max(cnt[j][e] for e in p)))
            room = ES // _p2(len(sp))
            for i, p in enumerate(sp):
                each = room // _p2(len(p))
                for kind in (0, 1):
                    src = c0 if k == "Z" else relay[(j, k)][kind]
                    items = []
                    for m, e in enumerate(p):
                        lo = i * room + m * each
                        eng = _bits(topo.mask(src, cores[e]))[lo:lo + each]
                        assert len(eng) == each
                        a0, pos, w = win[(j, e)]
                        items.append((cores[e], a0, pos, w, eng, "arr"))
                        ranks[e]["arrive"] += each
                    calls.setdefault(src, []).append((kind, items))
    _CACHE["p"] = (ranks, calls, waits)
    return _CACHE["p"]


def _issue(g, T, topo, core, calls):
    left = 0
    for kind, items in calls:
        ts = []
        for d, a0, pos, w, eng, mark in items:
            rid, pid = topo.addr(d, core)
            feed = mark == "fed"
            if kind == 0:
                src = T.q[:, a0:a0 + w].bitcast(dt.uint8)
                dst = (T.q if feed else T.lq)[:, pos:pos + w].bitcast(dt.uint8)
            else:
                src = T.s[:, a0:a0 + w]
                dst = (T.s if feed else T.ls)[:, pos:pos + w]
            ts.append(RemoteDMATransfer(dst_ids=[DstId(rid=rid, pnc=pid)], dma_engine_mask=sum(1 << x for x in eng),
                                        remote_sem=T.sem[mark], src=src, dst=dst))
            left += len(eng)
        g.remote_dma_fused(ts, local_sem=T.sem.sent)
    return left


def rank_program(g, core, T, topo):
    ranks, calls, waits = _plan(T, topo)
    rank = T.rank_of(core)
    if rank is None:
        if core in waits:
            g.wait_ge(T.sem.fed, waits[core])
            g.wait_ge(T.sem.sent, _issue(g, T, topo, core, calls[core]))
        return
    me = ranks[rank]
    g.sync.dma_start(T.xb[:, :], T.x[:, :]).then_inc(T.sem.ldx, 16)
    g.sync.dma_start(T.wb[:, :], T.w[:, :]).then_inc(T.sem.ldw, 16)
    g.vector.wait_ge(T.sem.ldx, 16)
    g.vector.quantize_mx(T.q[:, :], T.s[:, :], T.xb[:, :]).then_inc(T.sem.qx, 1)
    g.vector.wait_ge(T.sem.ldw, 16)
    g.vector.quantize_mx(T.wq[:, :], T.ws[:, :], T.wb[:, :]).then_inc(T.sem.qw, 1)
    g.wait_ge(T.sem.qx, 1)
    left = _issue(g, T, topo, core, calls[core])
    n = me["cols"]
    g.tensor.wait_ge(T.sem.qw, 1)
    g.tensor.wait_ge(T.sem.arr, me["arrive"])
    g.tensor.matmul_mx(T.ps[:, 0:n], T.wq[:, :], T.ws[:, :], T.lq[:, 0:n], T.ls[:, 0:n], True, True).then_inc(T.sem.mm, 1)
    g.vector.wait_ge(T.sem.mm, 1)
    for p, yo, c in me["copies"]:
        g.vector.tensor_copy(T.yb[:, yo:yo + c], T.ps[:, p:p + c]).then_inc(T.sem.cp, 1)
    g.sync.wait_ge(T.sem.cp, len(me["copies"]))
    g.sync.dma_start(T.y[:, :], T.yb[:, :]).then_inc(T.sem.st, 16)
    g.sync.wait_ge(T.sem.st, 16)
    g.wait_ge(T.sem.sent, left)
